import numpy as np
CORES = [7,135,263,391,15,143,271,399,23,151,279,407,31,159,287,415]
N = 16
def setup_inputs(rng):
    return {"x1": rng.standard_normal((N, 128, 32), dtype=np.float32), "x2": rng.standard_normal((N, 128, 1), dtype=np.float32), "x3": rng.standard_normal((N, 128, 128), dtype=np.float32), "x4": rng.standard_normal((N, 128, 8), dtype=np.float32)}
def reference(x1, x2, x3, x4):
    out = {}
    s = x1.sum(axis=0, dtype=np.float64).astype(x1.dtype)
    out["y1"] = np.broadcast_to(s, (N,) + s.shape)
    s = x2.sum(axis=0, dtype=np.float64).astype(x2.dtype)
    out["y2"] = np.broadcast_to(s, (N,) + s.shape)
    s = x3.sum(axis=0, dtype=np.float64).astype(x3.dtype)
    out["y3"] = np.broadcast_to(s, (N,) + s.shape)
    s = x4.sum(axis=0, dtype=np.float64).astype(x4.dtype)
    out["y4"] = np.broadcast_to(s, (N,) + s.shape)
    return out

from concourse.bass import DstId, RemoteDMATransfer

SCRATCH = {
    "Ua": ("dram", [8, 128, 16], "float32"),
    "Ub": ("dram", [8, 128, 4], "float32"),
    "Uc": ("dram", [16, 128, 1], "float32"),
    "Va": ("dram", [8, 128, 16], "float32"),
    "Vb": ("dram", [8, 128, 4], "float32"),
    "Vc": ("dram", [9, 128, 1], "float32"),
}
SEMAPHORES = ["ld", "got", "far", "res", "snt", "st"]

RANK_CORE, OWNER_CORE = 7, 3
X2_OWNER = 0
CABLE_MASK = {"a": 0x0F, "b": 0x10, "c": 0x20, "x2": 0x40}
GATHER_MASK = {"a": 0xFF, "b": 0x0F, "c": 0x10, "x2": 0x20}


def bits(m):
    return bin(m).count("1")


def index_of(host, chip):
    return chip + 4 * (0 if host in (0, 3) else 1)


def rank_program(g, core, T, topo):
    S = T.sem
    h, c = topo.host(core), topo.chip(core)
    if c > 3 or core % 8 not in (RANK_CORE, OWNER_CORE):
        return
    me = index_of(h, c)
    base = {}
    for hh in range(4):
        if topo.rack(hh) == topo.rack(h):
            for cc in range(4):
                base[index_of(hh, cc)] = hh * 128 + cc * 8

    def did(d):
        rid, pid = topo.addr(d, core)
        return DstId(rid=rid, pnc=pid)

    if core % 8 == RANK_CORE:
        g.sync.dma_start(T.Ua[:], T.x3[:, :]).then_inc(S.ld, 16)
        g.scalar.dma_start(T.Ub[:], T.x1[:, :]).then_inc(S.ld, 16)
        g.sync.dma_start(T.Uc[8], T.x2[:, :]).then_inc(S.ld, 16)
        g.scalar.dma_start(T.Uc[0:8], T.x4[:, :]).then_inc(S.ld, 16)
        g.wait_ge(S.ld, 64)

        sent = 0
        for k in ("a", "b", "c"):
            U = T["U" + k]
            pieces = [(j, j, me) for j in range(8)]
            if k == "c":
                pieces.append((8, X2_OWNER, 8 + me))
            off, on, trs = 0, 8, []
            for p, o, s in pieces:
                if o == me:
                    e, on = on, on + 1
                else:
                    e, off = off, off + 1
                trs.append(RemoteDMATransfer(dst_ids=[did(base[o] + OWNER_CORE)], dma_engine_mask=1 << e,
                                             remote_sem=S.got, src=U[p], dst=U[s], alu_op=0))
            g.remote_dma_fused(trs, local_sem=S.snt)
            sent += len(trs)

        total = 8 * (bits(GATHER_MASK["a"]) + bits(GATHER_MASK["b"]) + bits(GATHER_MASK["c"])) + bits(GATHER_MASK["x2"])
        g.sync.wait_ge(S.res, total)
        g.scalar.wait_ge(S.res, total)
        g.sync.dma_start(T.y3[:, :], T.Va[:]).then_inc(S.st, 16)
        g.scalar.dma_start(T.y1[:, :], T.Vb[:]).then_inc(S.st, 16)
        g.sync.dma_start(T.y2[:, :], T.Vc[8]).then_inc(S.st, 16)
        g.scalar.dma_start(T.y4[:, :], T.Vc[0:8]).then_inc(S.st, 16)
        g.wait_ge(S.snt, sent)
        g.wait_ge(S.st, 64)
        return

    has_x2 = me == X2_OWNER
    far_owner = did((3 - h) * 128 + core % 128)
    ranks = [did(base[j] + RANK_CORE) for j in range(8)]
    jobs = {"a": [("a", 0, 0, me)], "b": [("b", 0, 0, me)], "c": [("c", 0, 0, me)]}
    if has_x2:
        jobs["c"].append(("x2", 8, 1, 8))

    g.wait_ge(S.got, 8 * (4 if has_x2 else 3))
    sent = 0
    for k in ("a", "b", "c"):
        U, V = T["U" + k], T["V" + k]
        g.remote_dma_fused([RemoteDMATransfer(dst_ids=[far_owner], dma_engine_mask=CABLE_MASK[m], remote_sem=S.far,
                                              srcs=[U[s0 + s] for s in range(8)], dsts=[V[f]], alu_op=1)
                            for m, s0, f, p in jobs[k]], local_sem=S.snt)
        sent += sum(bits(CABLE_MASK[m]) for m, s0, f, p in jobs[k])
    g.wait_ge(S.far, sent)

    for k in ("a", "b", "c"):
        U, V = T["U" + k], T["V" + k]
        g.remote_dma_fused([RemoteDMATransfer(dst_ids=ranks, dma_engine_mask=GATHER_MASK[m], remote_sem=S.res,
                                              srcs=[U[s0 + s] for s in range(8)] + [V[f]], dsts=[V[p]] * 8, alu_op=1)
                            for m, s0, f, p in jobs[k]], local_sem=S.snt)
        sent += sum(bits(GATHER_MASK[m]) for m, s0, f, p in jobs[k])
    g.wait_ge(S.snt, sent)
